import numpy as np
import ml_dtypes


def mxq(x, axis, fmt="e4m3"):
    dtype, down = {"e4m3": (ml_dtypes.float8_e4m3fn, 7), "e5m2": (ml_dtypes.float8_e5m2, 14)}[fmt]
    v = np.moveaxis(np.asarray(x, np.float32).astype(ml_dtypes.bfloat16).astype(np.float64), axis, -1)
    blocks = v.reshape(v.shape[:-1] + (-1, 32))
    amax = np.abs(blocks).max(-1, keepdims=True)
    byte = np.maximum(np.where(amax > 0, np.frexp(amax)[1] - 1 + 127, 0) - down, 1)
    scale = np.exp2(byte - 127.0)
    codes = (blocks / scale).astype(np.float32).astype(dtype).astype(np.float64)
    return np.moveaxis((codes * scale).reshape(v.shape), -1, axis)


WIDE = False


def mx_kscale(k):
    if not WIDE:
        return np.ones(k)
    levels = np.array([10, -10, 5, -5, 0])
    if k % 512:
        return np.exp2(np.random.permutation(np.resize(levels, k // 32))).repeat(32)
    a = np.empty((k // 512, 16))
    for p in range(k // 512):
        a[p, :8] = np.random.permutation(np.resize(levels, 8))
        for g in range(8):
            far = levels[np.abs(levels - a[p, g]) >= 10]
            a[p, g + 8] = far[np.random.randint(len(far))]
    return np.exp2(a.ravel()).repeat(32)


def f64(x):
    return np.asarray(x).astype(np.float64)


def striped(idx):
    return np.tile(np.asarray(idx).reshape(-1, 16).T, (8, 1)).astype(np.uint16)


def unstriped(offs):
    return offs[:16].T.reshape(-1).astype(np.int64)


E2M1 = np.array([0.0, 0.5, 1.0, 1.5, 2.0, 3.0, 4.0, 6.0, -0.0, -0.5, -1.0, -1.5, -2.0, -3.0, -4.0, -6.0])


def pack_weight(w, fmt):
    k, n = w.shape
    w = f64(np.asarray(w, np.float32).astype(ml_dtypes.bfloat16)).reshape(k // 32, 32, n)
    amax = np.abs(w).max(1)
    if fmt == "e4m3":
        byte = np.frexp(amax)[1] - 1 + 127 - 7
    else:
        mant, ex = np.frexp(amax / 6.0)
        byte = np.where(mant > 0.5, ex, ex - 1) + 127
    byte = np.clip(np.where(amax > 0, byte, 1), 1, 254)
    scaled = (w * np.exp2(127.0 - byte)[:, None, :]).reshape(k, n).astype(np.float32)
    by_word = np.ascontiguousarray(scaled.reshape(k // 512, 128, 4, n).transpose(0, 1, 3, 2))
    if fmt == "e4m3":
        words = by_word.astype(ml_dtypes.float8_e4m3fn).view(np.uint8)
    else:
        c = by_word.astype(ml_dtypes.float4_e2m1fn).view(np.uint8) & 0xF
        words = (c[..., 0::2] | (c[..., 1::2] << 4)).reshape(k // 512, 128, 2 * n)
    return np.ascontiguousarray(words), np.ascontiguousarray(byte.astype(np.uint8).reshape(k // 512, 16, n))


def unpack_weight(words, scales, fmt):
    g, _, n = scales.shape
    words = np.ascontiguousarray(words).reshape(g, 128, n, -1)
    if fmt == "e4m3":
        vals = words.view(ml_dtypes.float8_e4m3fn).astype(np.float64)
    else:
        nib = np.empty((g, 128, n, 4), np.uint8)
        nib[..., 0::2] = words & 0xF
        nib[..., 1::2] = words >> 4
        vals = E2M1[nib]
    vals = vals * np.repeat(np.exp2(scales.astype(np.float64) - 127.0), 8, axis=1)[..., None]
    return vals.transpose(0, 1, 3, 2).reshape(g * 512, n)


def bf(x):
    return np.asarray(x, np.float32).astype(ml_dtypes.bfloat16)


def planes(Y):
    r, m = Y.shape
    b = f64(bf(Y)).reshape(r // 32, 32, m)
    amax = np.abs(b).max(1)
    byte = np.clip(np.where(amax > 0, np.frexp(amax)[1] - 1 + 127 - 7, 1), 1, 254)
    codes = (b * np.exp2(127.0 - byte)[:, None, :]).reshape(r, m).astype(np.float32).astype(ml_dtypes.float8_e4m3fn).view(np.uint8)
    words = codes.reshape(r // 512, 128, 4, m).transpose(0, 1, 3, 2)
    return np.ascontiguousarray(words), np.ascontiguousarray(byte.astype(np.uint8).reshape(r // 512, 16, m))


D, T, I, Q, E, J, U = 512, 2048, 512, 256, 512, 256, 1024


def setup_inputs():
    n = np.random.standard_normal
    idx = np.random.permutation(T)[:I]
    idx2 = np.random.permutation(U)[:J]
    fd = mx_kscale(D)
    fi = mx_kscale(I)
    ti = np.ones(T)
    ti[idx] = fi
    keysp = pack_weight(n((D, T)) / fd[:, None], "e2m1")
    return {
        "query": (n((D, Q)) * 0.8 / np.sqrt(D) * fd[:, None]).astype(np.float32),
        "keys_words": keysp[0],
        "keys_scales": keysp[1],
        "kept": (n((D, U)) * 1.5 / np.sqrt(D) * fd[:, None]).astype(np.float32),
        "kw1": (np.random.uniform(0.4, 1.6, (1, J))).astype(np.float32),
        "lam": (np.random.uniform(0.3, 0.7, (1, Q))).astype(np.float32),
        "os": (np.random.uniform(4.0, 16.0, (1, I)) * fi).astype(np.float32),
        "vals": (n((E, T)) / ti).astype(np.float32),
        "offs": striped(idx),
        "offs2": striped(idx2),
    }


def reference(query, keys_words, keys_scales, kept, kw1, lam, os, vals, offs, offs2):
    idx = unstriped(offs)
    idx2 = unstriped(offs2)
    keysu = unpack_weight(keys_words, keys_scales, "e2m1")
    keysidxg = keysu[:, idx]
    queryq = mxq(f64(query), 0, "e4m3")
    a0 = keysidxg.T @ queryq
    keptidx2q = mxq(f64(kept)[:, idx2], 0, "e4m3")
    kk = keysidxg.T @ keptidx2q
    m1 = np.max(kk * f64(kw1), axis=1, keepdims=True)
    s0 = a0 - m1 * f64(lam)
    s = s0.T
    p = np.exp(s - np.max(s, axis=1, keepdims=True))
    w = p / np.sum(p, axis=1, keepdims=True)
    wo1 = w * f64(os)
    wt1 = wo1.T
    vt1 = f64(vals)[:, idx].T
    vt1q = mxq(vt1, 0, "e4m3")
    wt1q = mxq(wt1, 0, "e4m3")
    o = vt1q.T @ wt1q
    words, scales = planes(o)
    return o, words, scales

@@ -1,0 +1,281 @@
+from contextlib import ExitStack
+
+import concourse.mybir as mybir
+from concourse.masks import make_identity
+
+D, T, I, Q, E, J, U = 512, 2048, 512, 256, 512, 256, 1024
+FLOPS = 2 * D * I * Q + 2 * D * I * J + 2 * I * E * Q
+
+F32 = mybir.dt.float32
+BF16 = mybir.dt.bfloat16
+I32 = mybir.dt.int32
+U32 = mybir.dt.uint32
+U16 = mybir.dt.uint16
+U8 = mybir.dt.uint8
+FP8X4 = mybir.dt.float8_e4m3fn_x4
+FP4X4 = mybir.dt.float4_e2m1fn_x4
+ALU = mybir.AluOpType
+ACT = mybir.ActivationFunctionType
+AX = mybir.AxisListType
+
+P = 128
+PACK = 4
+
+
+def tile_attend_novel_soft_read_pl_kernel(
+    tc, query, keys_words, keys_scales, kept, kw1, lam, slot_factor, vals, offs, offs2, out_0, out_1, out_2
+):
+    nc = tc.nc
+    with ExitStack() as ctx:
+        sb = ctx.enter_context(tc.tile_pool(name="sb", bufs=1))
+        ps = ctx.enter_context(tc.psum_pool(name="ps", bufs=1))
+
+        def tile(shape, dtype, name):
+            return sb.tile(shape, dtype, name=name, align_bytes=64)
+
+        def bank(shape, tag, name):
+            return ps.tile(shape, F32, name=name, tag=tag)
+
+        def quantize(src, codes, scales):
+            nc.vector.quantize_mx(out=codes.bitcast(FP8X4), scales=scales, in_=src)
+
+        offs_t = tile([P, I // 16], U16, "offs_t")
+        offs2_t = tile([P, J // 16], U16, "offs2_t")
+        key_scale_pool = tile([P, T], U8, "key_scale_pool")
+        key_word_pool = tile([P, T], U16, "key_word_pool")
+        nc.vector.memset(key_scale_pool[:].bitcast(I32), 0)
+        warm = tile([P, 1], F32, "warm")
+        warm_out = tile([P, 1], F32, "warm_out")
+        nc.vector.memset(warm[:], 0.0)
+        for quad in range(4):
+            nc.scalar.dma_start(
+                key_scale_pool[32 * quad : 32 * quad + 4, :].bitcast(I32),
+                keys_scales[0, 4 * quad : 4 * quad + 4, :].bitcast(I32),
+            )
+        nc.scalar.activation(warm_out[:], warm[:], ACT.Exp)
+        nc.sync.dma_start(offs_t[:], offs)
+        nc.sync.dma_start(key_word_pool[:].bitcast(I32), keys_words[0].bitcast(I32))
+        q_raw = tile([P, PACK, Q], F32, "q_raw")
+        nc.sync.dma_start(q_raw[:], query.rearrange("(p t) q -> p t q", t=PACK))
+        nc.sync.dma_start(offs2_t[:], offs2)
+        kept_rows = kept.rearrange("(p t) u -> p t u", t=PACK)
+        kept_pool = [tile([P, U], F32, "kept_pool%d" % t) for t in range(PACK)]
+        for t in range(PACK):
+            nc.sync.dma_start(kept_pool[t][:], kept_rows[:, t, :])
+        kw_col = tile([P, 2], F32, "kw_col")
+        lam_col = tile([P, 2], F32, "lam_col")
+        os_col = tile([P, 4], F32, "os_col")
+        with nc.allow_non_contiguous_dma(reason="one weight to a partition"):
+            nc.sync.dma_start(kw_col[:], kw1.rearrange("o (c p) -> p (o c)", p=P))
+        nc.sync.dma_start(lam_col[:], lam.rearrange("o (p c) -> p (o c)", p=P))
+        nc.sync.dma_start(os_col[:], slot_factor.rearrange("o (p c) -> p (o c)", p=P))
+        val_rows = vals.rearrange("(p t) n -> p t n", t=PACK)
+        val_pool = [tile([P, T], F32, "val_pool%d" % t) for t in range(PACK)]
+        for t in range(PACK):
+            nc.sync.dma_start(val_pool[t][:], val_rows[:, t, :])
+
+        ident = tile([P, P], F32, "ident")
+        make_identity(nc, ident[:])
+
+        key_scales = tile([P, I], U8, "key_scales")
+        key_words = tile([P, I], U16, "key_words")
+        nc.vector.tensor_copy(key_scales[:], key_scale_pool[:].indirect(offs_t[:]))
+        nc.vector.tensor_copy(key_words[:], key_word_pool[:].indirect(offs_t[:]))
+
+        q_bf = tile([P, Q, PACK], BF16, "q_bf")
+        nc.scalar.copy(
+            q_bf[:].rearrange("p (c i) t -> p c t i", i=4),
+            q_raw[:].rearrange("p t (c i) -> p c t i", i=4),
+        )
+        q_codes = tile([P, Q], U32, "q_codes")
+        q_scales = tile([P, Q], U8, "q_scales")
+
+        kept_bf = tile([P, J, PACK], BF16, "kept_bf")
+        kept_codes = tile([P, J], U32, "kept_codes")
+        kept_scales = tile([P, J], U8, "kept_scales")
+        for t in range(PACK):
+            nc.vector.tensor_copy(kept_bf[:, :, t], kept_pool[t][:].indirect(offs2_t[:]))
+            if t == 1:
+                quantize(q_bf[:].rearrange("p q t -> p (q t)"), q_codes[:], q_scales[:])
+
+        a0_sb = tile([P, 4, Q], F32, "a0_sb")
+        for half in range(2):
+            a0_ps = bank([P, 2, Q], "AB"[half], "a0_ps%d" % half)
+            for c2 in range(2):
+                c = 2 * half + c2
+                cols = slice(P * c, P * (c + 1))
+                nc.tensor.matmul_mx(
+                    out=a0_ps[:, c2, :],
+                    lhsT=key_words[:, cols].bitcast(FP4X4),
+                    lhsT_scale=key_scales[:, cols],
+                    rhs=q_codes[:].bitcast(FP8X4),
+                    rhs_scale=q_scales[:],
+                    start=True,
+                    stop=True,
+                )
+            nc.scalar.copy(a0_sb[:, 2 * half : 2 * half + 2, :], a0_ps[:])
+
+        s_ps = [bank([P, I], "S%d" % h, "s_ps%d" % h) for h in range(2)]
+        for h in range(2):
+            for c in range(4):
+                nc.tensor.matmul(
+                    s_ps[h][:, P * c : P * (c + 1)],
+                    lhsT=a0_sb[:, c, P * h : P * (h + 1)],
+                    rhs=ident[:],
+                    is_transpose=True,
+                    start=(c == 0),
+                    stop=False,
+                )
+
+        quantize(kept_bf[:].rearrange("p j t -> p (j t)"), kept_codes[:], kept_scales[:])
+
+        kk_ps = [bank([P, I], "CD"[c], "kk_ps%d" % c) for c in range(2)]
+        for c in range(2):
+            cols = slice(P * c, P * (c + 1))
+            nc.tensor.matmul_mx(
+                out=kk_ps[c][:],
+                lhsT=kept_codes[:, cols].bitcast(FP8X4),
+                lhsT_scale=kept_scales[:, cols],
+                rhs=key_words[:].bitcast(FP4X4),
+                rhs_scale=key_scales[:],
+                start=True,
+                stop=True,
+            )
+
+        lam_ps = bank([P, 2, P], "V", "lam_ps")
+        for c in range(2):
+            nc.tensor.transpose(lam_ps[:, c, :], lam_col[:, c : c + 1].to_broadcast([P, P]), ident[:])
+
+        kk0 = tile([P, I], F32, "kk0")
+        nc.scalar.activation(kk0[:], kk_ps[0][:], ACT.Copy, scale=kw_col[:, 0:1])
+        lam_row = tile([P, P, 2], F32, "lam_row")
+        nc.scalar.copy(lam_row[:], lam_ps[:].rearrange("p c n -> p n c"))
+        kmax = tile([P, I], F32, "kmax")
+        nc.vector.scalar_tensor_tensor(
+            out=kmax[:], in0=kk_ps[1][:], scalar=kw_col[:, 1:2], in1=kk0[:], op0=ALU.mult, op1=ALU.max
+        )
+        kmax_ps = bank([P, 4, P], "E", "kmax_ps")
+        for c in range(4):
+            nc.tensor.transpose(kmax_ps[:, c, :], kmax[:, P * c : P * (c + 1)], ident[:])
+        neg_m1 = tile([P, 4], F32, "neg_m1")
+        nc.vector.tensor_reduce(neg_m1[:], kmax_ps[:], axis=AX.X, op=ALU.max, negate=True)
+
+        penalty = tile([P, 4, Q], F32, "penalty")
+        lam_flat = lam_row[:].rearrange("p n c -> p (n c)")
+        for c in range(4):
+            if c < 2:
+                nc.vector.tensor_scalar(penalty[:, c, :], lam_flat, neg_m1[:, c : c + 1], None, op0=ALU.mult)
+            else:
+                nc.scalar.activation(penalty[:, c, :], lam_flat, ACT.Copy, scale=neg_m1[:, c : c + 1])
+        for h in range(2):
+            for c in range(4):
+                nc.tensor.matmul(
+                    s_ps[h][:, P * c : P * (c + 1)],
+                    lhsT=penalty[:, c, P * h : P * (h + 1)],
+                    rhs=ident[:],
+                    is_transpose=True,
+                    start=False,
+                    stop=(c == 3),
+                )
+
+        os_ps = bank([P, 4, P], "A", "os_ps")
+        for c in range(4):
+            nc.tensor.transpose(os_ps[:, c, :], os_col[:, c : c + 1].to_broadcast([P, P]), ident[:])
+        os_row = tile([P, P, 4], F32, "os_row")
+        nc.scalar.copy(os_row[:], os_ps[:].rearrange("p c n -> p n c"))
+
+        v_codes = [tile([P, P], U32, "v_codes%d" % t) for t in range(PACK)]
+        v_scales = [tile([P, P], U8, "v_scales%d" % t) for t in range(PACK)]
+
+        def turn_pairs(src_bf, dst_bf, tag, name):
+            words = src_bf.bitcast(F32)
+            turned = bank([P, 2, P], tag, name)
+            for u in range(2):
+                nc.tensor.transpose(turned[:, u, :], words[:, u : 2 * P : 2], ident[:])
+            nc.scalar.copy(
+                dst_bf.bitcast(F32).rearrange("p (m u) -> p m u", u=2),
+                turned[:].rearrange("p u m -> p m u"),
+            )
+
+        def values(t):
+            v_bf = tile([P, I], BF16, "v_bf%d" % t)
+            nc.vector.tensor_copy(v_bf[:], val_pool[t][:].indirect(offs_t[:]))
+            vt_bf = tile([P, I], BF16, "vt_bf%d" % t)
+            turn_pairs(v_bf[:], vt_bf[:], "V", "v_ps%d" % t)
+            quantize(vt_bf[:], v_codes[t][:], v_scales[t][:])
+
+        values(0)
+
+        w_codes = [tile([P, P], U32, "w_codes%d" % h) for h in range(2)]
+        w_scales = [tile([P, P], U8, "w_scales%d" % h) for h in range(2)]
+        neg_max = [tile([P, 1], F32, "neg_max%d" % h) for h in range(2)]
+        row_sum = [tile([P, 1], F32, "row_sum%d" % h) for h in range(2)]
+        inv_sum = [tile([P, 1], F32, "inv_sum%d" % h) for h in range(2)]
+        p_sb = [tile([P, I], F32, "p_sb%d" % h) for h in range(2)]
+        for h in range(2):
+            nc.vector.tensor_reduce(neg_max[h][:], s_ps[h][:], axis=AX.X, op=ALU.max, negate=True)
+            nc.scalar.activation(p_sb[h][:], s_ps[h][:], ACT.Exp, bias=neg_max[h][:], accum_out=row_sum[h][:])
+        values(1)
+        for h in range(2):
+            nc.vector.reciprocal(inv_sum[h][:], row_sum[h][:])
+            w_bf = tile([P, I], BF16, "w_bf%d" % h)
+            nc.vector.scalar_tensor_tensor(
+                out=w_bf[:],
+                in0=p_sb[h][:],
+                scalar=inv_sum[h][:],
+                in1=os_row[:].rearrange("p n c -> p (n c)"),
+                op0=ALU.mult,
+                op1=ALU.mult,
+            )
+            wt_bf = tile([P, I], BF16, "wt_bf%d" % h)
+            turn_pairs(w_bf[:], wt_bf[:], "CD"[h], "w_ps%d" % h)
+            quantize(wt_bf[:], w_codes[h][:], w_scales[h][:])
+        values(2)
+
+        o_sb = tile([P, PACK, Q], F32, "o_sb")
+        o_bf = tile([P, Q, PACK], BF16, "o_bf")
+        o_codes = tile([P, Q], U32, "o_codes")
+        o_scales = tile([P, Q], U8, "o_scales")
+
+        def product(dst, t, h):
+            nc.tensor.matmul_mx(
+                out=dst,
+                lhsT=v_codes[t][:].bitcast(FP8X4),
+                lhsT_scale=v_scales[t][:],
+                rhs=w_codes[h][:].bitcast(FP8X4),
+                rhs_scale=w_scales[h][:],
+                start=True,
+                stop=True,
+            )
+
+        out_rows = out_0.rearrange("(p t) q -> p t q", t=PACK)
+        for h in range(2):
+            early = bank([P, 3, P], "AB"[h], "early%d" % h)
+            for t in range(3):
+                product(early[:, t, :], t, h)
+            nc.scalar.copy(o_sb[:, 0:3, P * h : P * (h + 1)], early[:])
+        nc.sync.dma_start(out_rows[:, 0:3, :], o_sb[:, 0:3, :])
+
+        values(3)
+        for h in range(2):
+            late = bank([P, P], ("E", "S0")[h], "late%d" % h)
+            product(late[:], 3, h)
+            cols = slice(P * h, P * (h + 1))
+            nc.scalar.copy(o_sb[:, 3, cols], late[:])
+        for h in range(2):
+            cols = slice(P * h, P * (h + 1))
+            nc.vector.tensor_copy(
+                o_bf[:, cols, :].rearrange("p (c i) t -> p c t i", i=4),
+                o_sb[:, :, cols].rearrange("p t (c i) -> p c t i", i=4),
+            )
+        nc.sync.dma_start(out_rows[:, 3, :], o_sb[:, 3, :])
+        for h in range(2):
+            cols = slice(P * h, P * (h + 1))
+            quantize(o_bf[:, cols, :].rearrange("p q t -> p (q t)"), o_codes[:, cols], o_scales[:, cols])
+        nc.sync.dma_start(out_1[0].rearrange("p q r -> p (q r)").bitcast(I32), o_codes[:].bitcast(I32))
+        for quad in range(4):
+            queue = nc.sync if quad < 2 else nc.scalar
+            queue.dma_start(
+                out_2[0, 4 * quad : 4 * quad + 4, :].bitcast(I32),
+                o_scales[32 * quad : 32 * quad + 4, :].bitcast(I32),
+            )

@@ -30,8 +30,8 @@ def tile_attend_novel_soft_read_pl_kernel(
         sb = ctx.enter_context(tc.tile_pool(name="sb", bufs=1))
         ps = ctx.enter_context(tc.psum_pool(name="ps", bufs=1))
 
-        def tile(shape, dtype, name):
-            return sb.tile(shape, dtype, name=name, align_bytes=64)
+        def tile(shape, dtype, name, tag=None):
+            return sb.tile(shape, dtype, name=name, tag=tag or name, align_bytes=64)
 
         def bank(shape, tag, name):
             return ps.tile(shape, F32, name=name, tag=tag)
@@ -43,7 +43,7 @@ def tile_attend_novel_soft_read_pl_kernel(
         offs2_t = tile([P, J // 16], U16, "offs2_t")
         key_scale_pool = tile([P, T], U8, "key_scale_pool")
         key_word_pool = tile([P, T], U16, "key_word_pool")
-        nc.vector.memset(key_scale_pool[:].bitcast(I32), 0)
+        nc.gpsimd.memset(key_scale_pool[:].bitcast(I32), 0)
         warm = tile([P, 1], F32, "warm")
         warm_out = tile([P, 1], F32, "warm_out")
         nc.vector.memset(warm[:], 0.0)
@@ -52,23 +52,19 @@ def tile_attend_novel_soft_read_pl_kernel(
                 key_scale_pool[32 * quad : 32 * quad + 4, :].bitcast(I32),
                 keys_scales[0, 4 * quad : 4 * quad + 4, :].bitcast(I32),
             )
-        nc.scalar.activation(warm_out[:], warm[:], ACT.Exp)
+        kw_col = tile([P, 2], F32, "kw_col")
+        lam_col = tile([P, 2], F32, "lam_col")
+        os_col = tile([P, 4], F32, "os_col")
         nc.sync.dma_start(offs_t[:], offs)
         nc.sync.dma_start(key_word_pool[:].bitcast(I32), keys_words[0].bitcast(I32))
-        q_raw = tile([P, PACK, Q], F32, "q_raw")
-        nc.sync.dma_start(q_raw[:], query.rearrange("(p t) q -> p t q", t=PACK))
         nc.sync.dma_start(offs2_t[:], offs2)
         kept_rows = kept.rearrange("(p t) u -> p t u", t=PACK)
         kept_pool = [tile([P, U], F32, "kept_pool%d" % t) for t in range(PACK)]
         for t in range(PACK):
             nc.sync.dma_start(kept_pool[t][:], kept_rows[:, t, :])
-        kw_col = tile([P, 2], F32, "kw_col")
-        lam_col = tile([P, 2], F32, "lam_col")
-        os_col = tile([P, 4], F32, "os_col")
-        with nc.allow_non_contiguous_dma(reason="one weight to a partition"):
-            nc.sync.dma_start(kw_col[:], kw1.rearrange("o (c p) -> p (o c)", p=P))
-        nc.sync.dma_start(lam_col[:], lam.rearrange("o (p c) -> p (o c)", p=P))
-        nc.sync.dma_start(os_col[:], slot_factor.rearrange("o (p c) -> p (o c)", p=P))
+        nc.scalar.activation(warm_out[:], warm[:], ACT.Exp)
+        q_raw = tile([P, PACK, Q], F32, "q_raw")
+        nc.sync.dma_start(q_raw[:], query.rearrange("(p t) q -> p t q", t=PACK))
         val_rows = vals.rearrange("(p t) n -> p t n", t=PACK)
         val_pool = [tile([P, T], F32, "val_pool%d" % t) for t in range(PACK)]
         for t in range(PACK):
@@ -76,11 +72,46 @@ def tile_attend_novel_soft_read_pl_kernel(
 
         ident = tile([P, P], F32, "ident")
         make_identity(nc, ident[:])
+        nc.scalar.dma_start(lam_col[:], lam.rearrange("o (p c) -> p (o c)", p=P))
+        nc.scalar.dma_start(os_col[:], slot_factor.rearrange("o (p c) -> p (o c)", p=P))
+        with nc.allow_non_contiguous_dma(reason="one weight to a partition"):
+            nc.scalar.dma_start(kw_col[:], kw1.rearrange("o (c p) -> p (o c)", p=P))
+
+        lam_ps = bank([P, 2, P], "V", "lam_ps")
+        for c in range(2):
+            nc.tensor.transpose(lam_ps[:, c, :], lam_col[:, c : c + 1].to_broadcast([P, P]), ident[:])
+        lam_row = tile([P, P, 2], F32, "lam_row")
+        nc.scalar.copy(lam_row[:], lam_ps[:].rearrange("p c n -> p n c"))
+        os_ps = bank([P, 4, P], "E", "os_ps")
+        for c in range(4):
+            nc.tensor.transpose(os_ps[:, c, :], os_col[:, c : c + 1].to_broadcast([P, P]), ident[:])
+        os_row = tile([P, P, 4], F32, "os_row")
+        nc.scalar.copy(os_row[:], os_ps[:].rearrange("p c n -> p n c"))
 
         key_scales = tile([P, I], U8, "key_scales")
         key_words = tile([P, I], U16, "key_words")
-        nc.vector.tensor_copy(key_scales[:], key_scale_pool[:].indirect(offs_t[:]))
         nc.vector.tensor_copy(key_words[:], key_word_pool[:].indirect(offs_t[:]))
+        nc.vector.tensor_copy(key_scales[:], key_scale_pool[:].indirect(offs_t[:]))
+
+        kept_bf = tile([P, J, PACK], BF16, "kept_bf")
+        kept_codes = tile([P, J], U32, "kept_codes")
+        kept_scales = tile([P, J], U8, "kept_scales")
+        for t in range(PACK):
+            nc.vector.tensor_copy(kept_bf[:, :, t], kept_pool[t][:].indirect(offs2_t[:]))
+        quantize(kept_bf[:].rearrange("p j t -> p (j t)"), kept_codes[:], kept_scales[:])
+
+        kk_ps = [bank([P, I], "CD"[c], "kk_ps%d" % c) for c in range(2)]
+        for c in range(2):
+            cols = slice(P * c, P * (c + 1))
+            nc.tensor.matmul_mx(
+                out=kk_ps[c][:],
+                lhsT=kept_codes[:, cols].bitcast(FP8X4),
+                lhsT_scale=kept_scales[:, cols],
+                rhs=key_words[:].bitcast(FP4X4),
+                rhs_scale=key_scales[:],
+                start=True,
+                stop=True,
+            )
 
         q_bf = tile([P, Q, PACK], BF16, "q_bf")
         nc.scalar.copy(
@@ -89,15 +120,14 @@ def tile_attend_novel_soft_read_pl_kernel(
         )
         q_codes = tile([P, Q], U32, "q_codes")
         q_scales = tile([P, Q], U8, "q_scales")
+        quantize(q_bf[:].rearrange("p q t -> p (q t)"), q_codes[:], q_scales[:])
 
-        kept_bf = tile([P, J, PACK], BF16, "kept_bf")
-        kept_codes = tile([P, J], U32, "kept_codes")
-        kept_scales = tile([P, J], U8, "kept_scales")
-        for t in range(PACK):
-            nc.vector.tensor_copy(kept_bf[:, :, t], kept_pool[t][:].indirect(offs2_t[:]))
-            if t == 1:
-                quantize(q_bf[:].rearrange("p q t -> p (q t)"), q_codes[:], q_scales[:])
-
+        kk0 = tile([P, I], F32, "kk0")
+        nc.scalar.activation(kk0[:], kk_ps[0][:], ACT.Copy, scale=kw_col[:, 0:1])
+        kmax = tile([P, I], F32, "kmax")
+        nc.vector.scalar_tensor_tensor(
+            out=kmax[:], in0=kk_ps[1][:], scalar=kw_col[:, 1:2], in1=kk0[:], op0=ALU.mult, op1=ALU.max
+        )
         a0_sb = tile([P, 4, Q], F32, "a0_sb")
         for half in range(2):
             a0_ps = bank([P, 2, Q], "AB"[half], "a0_ps%d" % half)
@@ -115,76 +145,6 @@ def tile_attend_novel_soft_read_pl_kernel(
                 )
             nc.scalar.copy(a0_sb[:, 2 * half : 2 * half + 2, :], a0_ps[:])
 
-        s_ps = [bank([P, I], "S%d" % h, "s_ps%d" % h) for h in range(2)]
-        for h in range(2):
-            for c in range(4):
-                nc.tensor.matmul(
-                    s_ps[h][:, P * c : P * (c + 1)],
-                    lhsT=a0_sb[:, c, P * h : P * (h + 1)],
-                    rhs=ident[:],
-                    is_transpose=True,
-                    start=(c == 0),
-                    stop=False,
-                )
-
-        quantize(kept_bf[:].rearrange("p j t -> p (j t)"), kept_codes[:], kept_scales[:])
-
-        kk_ps = [bank([P, I], "CD"[c], "kk_ps%d" % c) for c in range(2)]
-        for c in range(2):
-            cols = slice(P * c, P * (c + 1))
-            nc.tensor.matmul_mx(
-                out=kk_ps[c][:],
-                lhsT=kept_codes[:, cols].bitcast(FP8X4),
-                lhsT_scale=kept_scales[:, cols],
-                rhs=key_words[:].bitcast(FP4X4),
-                rhs_scale=key_scales[:],
-                start=True,
-                stop=True,
-            )
-
-        lam_ps = bank([P, 2, P], "V", "lam_ps")
-        for c in range(2):
-            nc.tensor.transpose(lam_ps[:, c, :], lam_col[:, c : c + 1].to_broadcast([P, P]), ident[:])
-
-        kk0 = tile([P, I], F32, "kk0")
-        nc.scalar.activation(kk0[:], kk_ps[0][:], ACT.Copy, scale=kw_col[:, 0:1])
-        lam_row = tile([P, P, 2], F32, "lam_row")
-        nc.scalar.copy(lam_row[:], lam_ps[:].rearrange("p c n -> p n c"))
-        kmax = tile([P, I], F32, "kmax")
-        nc.vector.scalar_tensor_tensor(
-            out=kmax[:], in0=kk_ps[1][:], scalar=kw_col[:, 1:2], in1=kk0[:], op0=ALU.mult, op1=ALU.max
-        )
-        kmax_ps = bank([P, 4, P], "E", "kmax_ps")
-        for c in range(4):
-            nc.tensor.transpose(kmax_ps[:, c, :], kmax[:, P * c : P * (c + 1)], ident[:])
-        neg_m1 = tile([P, 4], F32, "neg_m1")
-        nc.vector.tensor_reduce(neg_m1[:], kmax_ps[:], axis=AX.X, op=ALU.max, negate=True)
-
-        penalty = tile([P, 4, Q], F32, "penalty")
-        lam_flat = lam_row[:].rearrange("p n c -> p (n c)")
-        for c in range(4):
-            if c < 2:
-                nc.vector.tensor_scalar(penalty[:, c, :], lam_flat, neg_m1[:, c : c + 1], None, op0=ALU.mult)
-            else:
-                nc.scalar.activation(penalty[:, c, :], lam_flat, ACT.Copy, scale=neg_m1[:, c : c + 1])
-        for h in range(2):
-            for c in range(4):
-                nc.tensor.matmul(
-                    s_ps[h][:, P * c : P * (c + 1)],
-                    lhsT=penalty[:, c, P * h : P * (h + 1)],
-                    rhs=ident[:],
-                    is_transpose=True,
-                    start=False,
-                    stop=(c == 3),
-                )
-
-        os_ps = bank([P, 4, P], "A", "os_ps")
-        for c in range(4):
-            nc.tensor.transpose(os_ps[:, c, :], os_col[:, c : c + 1].to_broadcast([P, P]), ident[:])
-        os_row = tile([P, P, 4], F32, "os_row")
-        nc.scalar.copy(os_row[:], os_ps[:].rearrange("p c n -> p n c"))
-
-        v_codes = [tile([P, P], U32, "v_codes%d" % t) for t in range(PACK)]
         v_scales = [tile([P, P], U8, "v_scales%d" % t) for t in range(PACK)]
 
         def turn_pairs(src_bf, dst_bf, tag, name):
@@ -197,40 +157,93 @@ def tile_attend_novel_soft_read_pl_kernel(
                 turned[:].rearrange("p u m -> p m u"),
             )
 
-        def values(t):
-            v_bf = tile([P, I], BF16, "v_bf%d" % t)
+        def gather_values(t):
+            v_bf = tile([P, I], BF16, "v_bf%d" % t, tag=("kk0", None, None)[t])
             nc.vector.tensor_copy(v_bf[:], val_pool[t][:].indirect(offs_t[:]))
-            vt_bf = tile([P, I], BF16, "vt_bf%d" % t)
+            return v_bf
+
+        def turn_values(t, v_bf):
+            vt_bf = tile([P, I], BF16, "vt_bf%d" % t, tag=("lam_row", "neg_max1", None)[t])
             turn_pairs(v_bf[:], vt_bf[:], "V", "v_ps%d" % t)
-            quantize(vt_bf[:], v_codes[t][:], v_scales[t][:])
+            return vt_bf
 
-        values(0)
+        kmax_ps = bank([P, 4, P], "E", "kmax_ps")
+        for c in range(4):
+            nc.tensor.transpose(kmax_ps[:, c, :], kmax[:, P * c : P * (c + 1)], ident[:])
+        s_ps = [bank([P, I], "DE"[h], "s_ps%d" % h) for h in range(2)]
+        for h in range(2):
+            for c in range(4):
+                nc.tensor.matmul(
+                    s_ps[h][:, P * c : P * (c + 1)],
+                    lhsT=a0_sb[:, c, P * h : P * (h + 1)],
+                    rhs=ident[:],
+                    is_transpose=True,
+                    start=(c == 0),
+                    stop=False,
+                )
 
-        w_codes = [tile([P, P], U32, "w_codes%d" % h) for h in range(2)]
+        v_bf0 = gather_values(0)
+        neg_m1 = tile([P, 4], F32, "neg_m1", tag="val_pool0")
+        nc.vector.tensor_reduce(neg_m1[:], kmax_ps[:], axis=AX.X, op=ALU.max, negate=True)
+
+        penalty = tile([P, 4, Q], F32, "penalty")
+        lam_flat = lam_row[:].rearrange("p n c -> p (n c)")
+        for c in range(4):
+            if c < 2:
+                nc.vector.tensor_scalar(penalty[:, c, :], lam_flat, neg_m1[:, c : c + 1], None, op0=ALU.mult)
+            else:
+                nc.scalar.activation(penalty[:, c, :], lam_flat, ACT.Copy, scale=neg_m1[:, c : c + 1])
+        for c in range(4):
+            for h in range(2):
+                nc.tensor.matmul(
+                    s_ps[h][:, P * c : P * (c + 1)],
+                    lhsT=penalty[:, c, P * h : P * (h + 1)],
+                    rhs=ident[:],
+                    is_transpose=True,
+                    start=False,
+                    stop=(c == 3),
+                )
+
+        vt = [turn_values(0, v_bf0)]
+        v_bf1 = gather_values(1)
+
         w_scales = [tile([P, P], U8, "w_scales%d" % h) for h in range(2)]
-        neg_max = [tile([P, 1], F32, "neg_max%d" % h) for h in range(2)]
+        neg_max = [tile([P, 1], F32, "neg_max%d" % h, tag=("val_pool1", None)[h]) for h in range(2)]
         row_sum = [tile([P, 1], F32, "row_sum%d" % h) for h in range(2)]
-        inv_sum = [tile([P, 1], F32, "inv_sum%d" % h) for h in range(2)]
         p_sb = [tile([P, I], F32, "p_sb%d" % h) for h in range(2)]
         for h in range(2):
             nc.vector.tensor_reduce(neg_max[h][:], s_ps[h][:], axis=AX.X, op=ALU.max, negate=True)
             nc.scalar.activation(p_sb[h][:], s_ps[h][:], ACT.Exp, bias=neg_max[h][:], accum_out=row_sum[h][:])
-        values(1)
+        vt.append(turn_values(1, v_bf1))
+        vt.append(turn_values(2, gather_values(2)))
+        inv_sum = [tile([P, 1], F32, "inv_sum%d" % h, tag=("val_pool2", None)[h]) for h in range(2)]
+        w_bf = [tile([P, I], BF16, "w_bf%d" % h) for h in range(2)]
         for h in range(2):
             nc.vector.reciprocal(inv_sum[h][:], row_sum[h][:])
-            w_bf = tile([P, I], BF16, "w_bf%d" % h)
             nc.vector.scalar_tensor_tensor(
-                out=w_bf[:],
+                out=w_bf[h][:],
                 in0=p_sb[h][:],
                 scalar=inv_sum[h][:],
                 in1=os_row[:].rearrange("p n c -> p (n c)"),
                 op0=ALU.mult,
                 op1=ALU.mult,
             )
-            wt_bf = tile([P, I], BF16, "wt_bf%d" % h)
-            turn_pairs(w_bf[:], wt_bf[:], "CD"[h], "w_ps%d" % h)
-            quantize(wt_bf[:], w_codes[h][:], w_scales[h][:])
-        values(2)
+        v_bf3 = tile([P, I], BF16, "v_bf3", tag="p_sb1")
+        nc.vector.tensor_copy(v_bf3[:], val_pool[3][:].indirect(offs_t[:]))
+        wt_bf = [tile([P, I], BF16, "wt_bf%d" % h, tag=None) for h in range(2)]
+        for h in range(2):
+            turn_pairs(w_bf[h][:], wt_bf[h][:], "S%d" % h, "w_ps%d" % h)
+        codes = tile([P, 6, P], U32, "codes", tag="val_pool3")
+        v_codes = [codes[:, t, :] for t in range(PACK)]
+        w_codes = [codes[:, PACK + h, :] for h in range(2)]
+        vt_bf3 = tile([P, I], BF16, "vt_bf3")
+        turn_pairs(v_bf3[:], vt_bf3[:], "V", "v_ps3")
+        vt.append(vt_bf3)
+        quantize(wt_bf[0][:], w_codes[0], w_scales[0][:])
+        for t in range(3):
+            quantize(vt[t][:], v_codes[t], v_scales[t][:])
+        quantize(wt_bf[1][:], w_codes[1], w_scales[1][:])
+        quantize(vt[3][:], v_codes[3], v_scales[3][:])
 
         o_sb = tile([P, PACK, Q], F32, "o_sb")
         o_bf = tile([P, Q, PACK], BF16, "o_bf")
@@ -240,38 +253,35 @@ def tile_attend_novel_soft_read_pl_kernel(
         def product(dst, t, h):
             nc.tensor.matmul_mx(
                 out=dst,
-                lhsT=v_codes[t][:].bitcast(FP8X4),
+                lhsT=v_codes[t].bitcast(FP8X4),
                 lhsT_scale=v_scales[t][:],
-                rhs=w_codes[h][:].bitcast(FP8X4),
+                rhs=w_codes[h].bitcast(FP8X4),
                 rhs_scale=w_scales[h][:],
                 start=True,
                 stop=True,
             )
 
         out_rows = out_0.rearrange("(p t) q -> p t q", t=PACK)
+        halves = [slice(0, P), slice(P, Q)]
+        copy_on = [nc.vector.tensor_copy, nc.scalar.copy]
+        early = [bank([P, 3, P], "AB"[h], "early%d" % h) for h in range(2)]
+        late = [bank([P, P], "CD"[h], "late%d" % h) for h in range(2)]
         for h in range(2):
-            early = bank([P, 3, P], "AB"[h], "early%d" % h)
             for t in range(3):
-                product(early[:, t, :], t, h)
-            nc.scalar.copy(o_sb[:, 0:3, P * h : P * (h + 1)], early[:])
+                product(early[h][:, t, :], t, h)
+        for h in range(2):
+            product(late[h][:], 3, h)
+        for h in range(2):
+            copy_on[h](o_sb[:, 0:3, halves[h]], early[h][:])
         nc.sync.dma_start(out_rows[:, 0:3, :], o_sb[:, 0:3, :])
-
-        values(3)
         for h in range(2):
-            late = bank([P, P], ("E", "S0")[h], "late%d" % h)
-            product(late[:], 3, h)
-            cols = slice(P * h, P * (h + 1))
-            nc.scalar.copy(o_sb[:, 3, cols], late[:])
+            copy_on[h](o_bf[:, halves[h], 0:3], early[h][:].rearrange("p t q -> p q t"))
         for h in range(2):
-            cols = slice(P * h, P * (h + 1))
-            nc.vector.tensor_copy(
-                o_bf[:, cols, :].rearrange("p (c i) t -> p c t i", i=4),
-                o_sb[:, :, cols].rearrange("p t (c i) -> p c t i", i=4),
-            )
-        nc.sync.dma_start(out_rows[:, 3, :], o_sb[:, 3, :])
-        for h in range(2):
-            cols = slice(P * h, P * (h + 1))
-            quantize(o_bf[:, cols, :].rearrange("p q t -> p (q t)"), o_codes[:, cols], o_scales[:, cols])
+            copy_on[h](o_bf[:, halves[h], 3], late[h][:])
+        quantize(o_bf[:].rearrange("p q t -> p (q t)"), o_codes[:], o_scales[:])
+        for h in (1, 0):
+            nc.scalar.copy(o_sb[:, 3, halves[h]], late[h][:])
+        nc.scalar.dma_start(out_rows[:, 3, :], o_sb[:, 3, :])
         nc.sync.dma_start(out_1[0].rearrange("p q r -> p (q r)").bitcast(I32), o_codes[:].bitcast(I32))
         for quad in range(4):
             queue = nc.sync if quad < 2 else nc.scalar

@@ -88,16 +88,17 @@ def tile_attend_novel_soft_read_pl_kernel(
         os_row = tile([P, P, 4], F32, "os_row")
         nc.scalar.copy(os_row[:], os_ps[:].rearrange("p c n -> p n c"))
 
-        key_scales = tile([P, I], U8, "key_scales")
         key_words = tile([P, I], U16, "key_words")
         nc.vector.tensor_copy(key_words[:], key_word_pool[:].indirect(offs_t[:]))
-        nc.vector.tensor_copy(key_scales[:], key_scale_pool[:].indirect(offs_t[:]))
 
         kept_bf = tile([P, J, PACK], BF16, "kept_bf")
         kept_codes = tile([P, J], U32, "kept_codes")
         kept_scales = tile([P, J], U8, "kept_scales")
         for t in range(PACK):
             nc.vector.tensor_copy(kept_bf[:, :, t], kept_pool[t][:].indirect(offs2_t[:]))
+            if t == 1:
+                key_scales = tile([P, I], U8, "key_scales")
+                nc.vector.tensor_copy(key_scales[:], key_scale_pool[:].indirect(offs_t[:]))
         quantize(kept_bf[:].rearrange("p j t -> p (j t)"), kept_codes[:], kept_scales[:])
 
         kk_ps = [bank([P, I], "CD"[c], "kk_ps%d" % c) for c in range(2)]
@@ -114,7 +115,7 @@ def tile_attend_novel_soft_read_pl_kernel(
             )
 
         q_bf = tile([P, Q, PACK], BF16, "q_bf")
-        nc.scalar.copy(
+        nc.vector.tensor_copy(
             q_bf[:].rearrange("p (c i) t -> p c t i", i=4),
             q_raw[:].rearrange("p t (c i) -> p c t i", i=4),
         )
@@ -124,11 +125,11 @@ def tile_attend_novel_soft_read_pl_kernel(
 
         kk0 = tile([P, I], F32, "kk0")
         nc.scalar.activation(kk0[:], kk_ps[0][:], ACT.Copy, scale=kw_col[:, 0:1])
-        kmax = tile([P, I], F32, "kmax")
+        kmax = tile([P, I], F32, "kmax", tag="q_bf")
         nc.vector.scalar_tensor_tensor(
             out=kmax[:], in0=kk_ps[1][:], scalar=kw_col[:, 1:2], in1=kk0[:], op0=ALU.mult, op1=ALU.max
         )
-        a0_sb = tile([P, 4, Q], F32, "a0_sb")
+        a0_sb = tile([P, 4, Q], F32, "a0_sb", tag="kk0")
         for half in range(2):
             a0_ps = bank([P, 2, Q], "AB"[half], "a0_ps%d" % half)
             for c2 in range(2):
@@ -158,7 +159,7 @@ def tile_attend_novel_soft_read_pl_kernel(
             )
 
         def gather_values(t):
-            v_bf = tile([P, I], BF16, "v_bf%d" % t, tag=("kk0", None, None)[t])
+            v_bf = tile([P, I], BF16, "v_bf%d" % t, tag=None)
             nc.vector.tensor_copy(v_bf[:], val_pool[t][:].indirect(offs_t[:]))
             return v_bf
 
@@ -170,7 +171,7 @@ def tile_attend_novel_soft_read_pl_kernel(
         kmax_ps = bank([P, 4, P], "E", "kmax_ps")
         for c in range(4):
             nc.tensor.transpose(kmax_ps[:, c, :], kmax[:, P * c : P * (c + 1)], ident[:])
-        s_ps = [bank([P, I], "DE"[h], "s_ps%d" % h) for h in range(2)]
+        s_ps = [bank([P, I], "S%d" % h, "s_ps%d" % h) for h in range(2)]
         for h in range(2):
             for c in range(4):
                 nc.tensor.matmul(
@@ -228,11 +229,11 @@ def tile_attend_novel_soft_read_pl_kernel(
                 op0=ALU.mult,
                 op1=ALU.mult,
             )
-        v_bf3 = tile([P, I], BF16, "v_bf3", tag="p_sb1")
+        v_bf3 = tile([P, I], BF16, "v_bf3")
         nc.vector.tensor_copy(v_bf3[:], val_pool[3][:].indirect(offs_t[:]))
         wt_bf = [tile([P, I], BF16, "wt_bf%d" % h, tag=None) for h in range(2)]
         for h in range(2):
-            turn_pairs(w_bf[h][:], wt_bf[h][:], "S%d" % h, "w_ps%d" % h)
+            turn_pairs(w_bf[h][:], wt_bf[h][:], "CD"[h], "w_ps%d" % h)
         codes = tile([P, 6, P], U32, "codes", tag="val_pool3")
         v_codes = [codes[:, t, :] for t in range(PACK)]
         w_codes = [codes[:, PACK + h, :] for h in range(2)]
@@ -265,17 +266,17 @@ def tile_attend_novel_soft_read_pl_kernel(
         halves = [slice(0, P), slice(P, Q)]
         copy_on = [nc.vector.tensor_copy, nc.scalar.copy]
         early = [bank([P, 3, P], "AB"[h], "early%d" % h) for h in range(2)]
-        late = [bank([P, P], "CD"[h], "late%d" % h) for h in range(2)]
+        late = [bank([P, P], ("E", "S0")[h], "late%d" % h) for h in range(2)]
         for h in range(2):
             for t in range(3):
                 product(early[h][:, t, :], t, h)
         for h in range(2):
             product(late[h][:], 3, h)
         for h in range(2):
-            copy_on[h](o_sb[:, 0:3, halves[h]], early[h][:])
+            nc.scalar.copy(o_sb[:, 0:3, halves[h]], early[h][:])
         nc.sync.dma_start(out_rows[:, 0:3, :], o_sb[:, 0:3, :])
-        for h in range(2):
-            copy_on[h](o_bf[:, halves[h], 0:3], early[h][:].rearrange("p t q -> p q t"))
+        nc.vector.tensor_copy(o_bf[:, halves[0], 0:3], o_sb[:, 0:3, halves[0]].rearrange("p t q -> p q t"))
+        nc.scalar.copy(o_bf[:, halves[1], 0:3], early[1][:].rearrange("p t q -> p q t"))
         for h in range(2):
             copy_on[h](o_bf[:, halves[h], 3], late[h][:])
         quantize(o_bf[:].rearrange("p q t -> p (q t)"), o_codes[:], o_scales[:])

@@ -44,9 +44,6 @@ def tile_attend_novel_soft_read_pl_kernel(
         key_scale_pool = tile([P, T], U8, "key_scale_pool")
         key_word_pool = tile([P, T], U16, "key_word_pool")
         nc.gpsimd.memset(key_scale_pool[:].bitcast(I32), 0)
-        warm = tile([P, 1], F32, "warm")
-        warm_out = tile([P, 1], F32, "warm_out")
-        nc.vector.memset(warm[:], 0.0)
         for quad in range(4):
             nc.scalar.dma_start(
                 key_scale_pool[32 * quad : 32 * quad + 4, :].bitcast(I32),
@@ -62,7 +59,6 @@ def tile_attend_novel_soft_read_pl_kernel(
         kept_pool = [tile([P, U], F32, "kept_pool%d" % t) for t in range(PACK)]
         for t in range(PACK):
             nc.sync.dma_start(kept_pool[t][:], kept_rows[:, t, :])
-        nc.scalar.activation(warm_out[:], warm[:], ACT.Exp)
         q_raw = tile([P, PACK, Q], F32, "q_raw")
         nc.sync.dma_start(q_raw[:], query.rearrange("(p t) q -> p t q", t=PACK))
         val_rows = vals.rearrange("(p t) n -> p t n", t=PACK)

from contextlib import ExitStack

import concourse.mybir as mybir
from concourse.masks import make_identity

D, T, I, Q, E, J, U = 512, 2048, 512, 256, 512, 256, 1024
FLOPS = 2 * D * I * Q + 2 * D * I * J + 2 * I * E * Q

F32 = mybir.dt.float32
BF16 = mybir.dt.bfloat16
I32 = mybir.dt.int32
U32 = mybir.dt.uint32
U16 = mybir.dt.uint16
U8 = mybir.dt.uint8
FP8X4 = mybir.dt.float8_e4m3fn_x4
FP4X4 = mybir.dt.float4_e2m1fn_x4
ALU = mybir.AluOpType
ACT = mybir.ActivationFunctionType
AX = mybir.AxisListType

P = 128
PACK = 4


def tile_attend_novel_soft_read_pl_kernel(
    tc, query, keys_words, keys_scales, kept, kw1, lam, slot_factor, vals, offs, offs2, out_0, out_1, out_2
):
    nc = tc.nc
    with ExitStack() as ctx:
        sb = ctx.enter_context(tc.tile_pool(name="sb", bufs=1))
        ps = ctx.enter_context(tc.psum_pool(name="ps", bufs=1))

        def tile(shape, dtype, name, tag=None):
            return sb.tile(shape, dtype, name=name, tag=tag or name, align_bytes=64)

        def bank(shape, tag, name):
            return ps.tile(shape, F32, name=name, tag=tag)

        def quantize(src, codes, scales):
            nc.vector.quantize_mx(out=codes.bitcast(FP8X4), scales=scales, in_=src)

        offs_t = tile([P, I // 16], U16, "offs_t")
        offs2_t = tile([P, J // 16], U16, "offs2_t")
        key_scale_pool = tile([P, T], U8, "key_scale_pool")
        key_word_pool = tile([P, T], U16, "key_word_pool")
        nc.gpsimd.memset(key_scale_pool[:].bitcast(I32), 0)
        for quad in range(4):
            nc.scalar.dma_start(
                key_scale_pool[32 * quad : 32 * quad + 4, :].bitcast(I32),
                keys_scales[0, 4 * quad : 4 * quad + 4, :].bitcast(I32),
            )
        kw_col = tile([P, 2], F32, "kw_col")
        lam_col = tile([P, 2], F32, "lam_col")
        os_col = tile([P, 4], F32, "os_col")
        nc.sync.dma_start(offs_t[:], offs)
        nc.sync.dma_start(key_word_pool[:].bitcast(I32), keys_words[0].bitcast(I32))
        nc.sync.dma_start(offs2_t[:], offs2)
        kept_rows = kept.rearrange("(p t) u -> p t u", t=PACK)
        kept_pool = [tile([P, U], F32, "kept_pool%d" % t) for t in range(PACK)]
        for t in range(PACK):
            nc.sync.dma_start(kept_pool[t][:], kept_rows[:, t, :])
        q_raw = tile([P, PACK, Q], F32, "q_raw")
        nc.sync.dma_start(q_raw[:], query.rearrange("(p t) q -> p t q", t=PACK))
        val_rows = vals.rearrange("(p t) n -> p t n", t=PACK)
        val_pool = [tile([P, T], F32, "val_pool%d" % t) for t in range(PACK)]
        for t in range(PACK):
            nc.sync.dma_start(val_pool[t][:], val_rows[:, t, :])

        ident = tile([P, P], F32, "ident")
        make_identity(nc, ident[:])
        nc.scalar.dma_start(lam_col[:], lam.rearrange("o (p c) -> p (o c)", p=P))
        nc.scalar.dma_start(os_col[:], slot_factor.rearrange("o (p c) -> p (o c)", p=P))
        with nc.allow_non_contiguous_dma(reason="one weight to a partition"):
            nc.scalar.dma_start(kw_col[:], kw1.rearrange("o (c p) -> p (o c)", p=P))

        lam_ps = bank([P, 2, P], "V", "lam_ps")
        for c in range(2):
            nc.tensor.transpose(lam_ps[:, c, :], lam_col[:, c : c + 1].to_broadcast([P, P]), ident[:])
        lam_row = tile([P, P, 2], F32, "lam_row")
        nc.scalar.copy(lam_row[:], lam_ps[:].rearrange("p c n -> p n c"))
        os_ps = bank([P, 4, P], "E", "os_ps")
        for c in range(4):
            nc.tensor.transpose(os_ps[:, c, :], os_col[:, c : c + 1].to_broadcast([P, P]), ident[:])
        os_row = tile([P, P, 4], F32, "os_row")
        nc.scalar.copy(os_row[:], os_ps[:].rearrange("p c n -> p n c"))

        key_words = tile([P, I], U16, "key_words")
        nc.vector.tensor_copy(key_words[:], key_word_pool[:].indirect(offs_t[:]))

        kept_bf = tile([P, J, PACK], BF16, "kept_bf")
        kept_codes = tile([P, J], U32, "kept_codes")
        kept_scales = tile([P, J], U8, "kept_scales")
        for t in range(PACK):
            nc.vector.tensor_copy(kept_bf[:, :, t], kept_pool[t][:].indirect(offs2_t[:]))
            if t == 1:
                key_scales = tile([P, I], U8, "key_scales")
                nc.vector.tensor_copy(key_scales[:], key_scale_pool[:].indirect(offs_t[:]))
        quantize(kept_bf[:].rearrange("p j t -> p (j t)"), kept_codes[:], kept_scales[:])

        kk_ps = [bank([P, I], "CD"[c], "kk_ps%d" % c) for c in range(2)]
        for c in range(2):
            cols = slice(P * c, P * (c + 1))
            nc.tensor.matmul_mx(
                out=kk_ps[c][:],
                lhsT=kept_codes[:, cols].bitcast(FP8X4),
                lhsT_scale=kept_scales[:, cols],
                rhs=key_words[:].bitcast(FP4X4),
                rhs_scale=key_scales[:],
                start=True,
                stop=True,
            )

        q_bf = tile([P, Q, PACK], BF16, "q_bf")
        nc.vector.tensor_copy(
            q_bf[:].rearrange("p (c i) t -> p c t i", i=4),
            q_raw[:].rearrange("p t (c i) -> p c t i", i=4),
        )
        q_codes = tile([P, Q], U32, "q_codes")
        q_scales = tile([P, Q], U8, "q_scales")
        quantize(q_bf[:].rearrange("p q t -> p (q t)"), q_codes[:], q_scales[:])

        kk0 = tile([P, I], F32, "kk0")
        nc.scalar.activation(kk0[:], kk_ps[0][:], ACT.Copy, scale=kw_col[:, 0:1])
        kmax = tile([P, I], F32, "kmax", tag="q_bf")
        nc.vector.scalar_tensor_tensor(
            out=kmax[:], in0=kk_ps[1][:], scalar=kw_col[:, 1:2], in1=kk0[:], op0=ALU.mult, op1=ALU.max
        )
        a0_sb = tile([P, 4, Q], F32, "a0_sb", tag="kk0")
        for half in range(2):
            a0_ps = bank([P, 2, Q], "AB"[half], "a0_ps%d" % half)
            for c2 in range(2):
                c = 2 * half + c2
                cols = slice(P * c, P * (c + 1))
                nc.tensor.matmul_mx(
                    out=a0_ps[:, c2, :],
                    lhsT=key_words[:, cols].bitcast(FP4X4),
                    lhsT_scale=key_scales[:, cols],
                    rhs=q_codes[:].bitcast(FP8X4),
                    rhs_scale=q_scales[:],
                    start=True,
                    stop=True,
                )
            nc.scalar.copy(a0_sb[:, 2 * half : 2 * half + 2, :], a0_ps[:])

        v_scales = [tile([P, P], U8, "v_scales%d" % t) for t in range(PACK)]

        def turn_pairs(src_bf, dst_bf, tag, name):
            words = src_bf.bitcast(F32)
            turned = bank([P, 2, P], tag, name)
            for u in range(2):
                nc.tensor.transpose(turned[:, u, :], words[:, u : 2 * P : 2], ident[:])
            nc.scalar.copy(
                dst_bf.bitcast(F32).rearrange("p (m u) -> p m u", u=2),
                turned[:].rearrange("p u m -> p m u"),
            )

        def gather_values(t):
            v_bf = tile([P, I], BF16, "v_bf%d" % t, tag=None)
            nc.vector.tensor_copy(v_bf[:], val_pool[t][:].indirect(offs_t[:]))
            return v_bf

        def turn_values(t, v_bf):
            vt_bf = tile([P, I], BF16, "vt_bf%d" % t, tag=("lam_row", "neg_max1", None)[t])
            turn_pairs(v_bf[:], vt_bf[:], "V", "v_ps%d" % t)
            return vt_bf

        kmax_ps = bank([P, 4, P], "E", "kmax_ps")
        for c in range(4):
            nc.tensor.transpose(kmax_ps[:, c, :], kmax[:, P * c : P * (c + 1)], ident[:])
        s_ps = [bank([P, I], "S%d" % h, "s_ps%d" % h) for h in range(2)]
        for h in range(2):
            for c in range(4):
                nc.tensor.matmul(
                    s_ps[h][:, P * c : P * (c + 1)],
                    lhsT=a0_sb[:, c, P * h : P * (h + 1)],
                    rhs=ident[:],
                    is_transpose=True,
                    start=(c == 0),
                    stop=False,
                )

        v_bf0 = gather_values(0)
        neg_m1 = tile([P, 4], F32, "neg_m1", tag="val_pool0")
        nc.vector.tensor_reduce(neg_m1[:], kmax_ps[:], axis=AX.X, op=ALU.max, negate=True)

        penalty = tile([P, 4, Q], F32, "penalty")
        lam_flat = lam_row[:].rearrange("p n c -> p (n c)")
        for c in range(4):
            if c < 2:
                nc.vector.tensor_scalar(penalty[:, c, :], lam_flat, neg_m1[:, c : c + 1], None, op0=ALU.mult)
            else:
                nc.scalar.activation(penalty[:, c, :], lam_flat, ACT.Copy, scale=neg_m1[:, c : c + 1])
        for c in range(4):
            for h in range(2):
                nc.tensor.matmul(
                    s_ps[h][:, P * c : P * (c + 1)],
                    lhsT=penalty[:, c, P * h : P * (h + 1)],
                    rhs=ident[:],
                    is_transpose=True,
                    start=False,
                    stop=(c == 3),
                )

        vt = [turn_values(0, v_bf0)]
        v_bf1 = gather_values(1)

        w_scales = [tile([P, P], U8, "w_scales%d" % h) for h in range(2)]
        neg_max = [tile([P, 1], F32, "neg_max%d" % h, tag=("val_pool1", None)[h]) for h in range(2)]
        row_sum = [tile([P, 1], F32, "row_sum%d" % h) for h in range(2)]
        p_sb = [tile([P, I], F32, "p_sb%d" % h) for h in range(2)]
        for h in range(2):
            nc.vector.tensor_reduce(neg_max[h][:], s_ps[h][:], axis=AX.X, op=ALU.max, negate=True)
            nc.scalar.activation(p_sb[h][:], s_ps[h][:], ACT.Exp, bias=neg_max[h][:], accum_out=row_sum[h][:])
        vt.append(turn_values(1, v_bf1))
        vt.append(turn_values(2, gather_values(2)))
        inv_sum = [tile([P, 1], F32, "inv_sum%d" % h, tag=("val_pool2", None)[h]) for h in range(2)]
        w_bf = [tile([P, I], BF16, "w_bf%d" % h) for h in range(2)]
        for h in range(2):
            nc.vector.reciprocal(inv_sum[h][:], row_sum[h][:])
            nc.vector.scalar_tensor_tensor(
                out=w_bf[h][:],
                in0=p_sb[h][:],
                scalar=inv_sum[h][:],
                in1=os_row[:].rearrange("p n c -> p (n c)"),
                op0=ALU.mult,
                op1=ALU.mult,
            )
        v_bf3 = tile([P, I], BF16, "v_bf3")
        nc.vector.tensor_copy(v_bf3[:], val_pool[3][:].indirect(offs_t[:]))
        wt_bf = [tile([P, I], BF16, "wt_bf%d" % h, tag=None) for h in range(2)]
        for h in range(2):
            turn_pairs(w_bf[h][:], wt_bf[h][:], "CD"[h], "w_ps%d" % h)
        codes = tile([P, 6, P], U32, "codes", tag="val_pool3")
        v_codes = [codes[:, t, :] for t in range(PACK)]
        w_codes = [codes[:, PACK + h, :] for h in range(2)]
        vt_bf3 = tile([P, I], BF16, "vt_bf3")
        turn_pairs(v_bf3[:], vt_bf3[:], "V", "v_ps3")
        vt.append(vt_bf3)
        quantize(wt_bf[0][:], w_codes[0], w_scales[0][:])
        for t in range(3):
            quantize(vt[t][:], v_codes[t], v_scales[t][:])
        quantize(wt_bf[1][:], w_codes[1], w_scales[1][:])
        quantize(vt[3][:], v_codes[3], v_scales[3][:])

        o_sb = tile([P, PACK, Q], F32, "o_sb")
        o_bf = tile([P, Q, PACK], BF16, "o_bf")
        o_codes = tile([P, Q], U32, "o_codes")
        o_scales = tile([P, Q], U8, "o_scales")

        def product(dst, t, h):
            nc.tensor.matmul_mx(
                out=dst,
                lhsT=v_codes[t].bitcast(FP8X4),
                lhsT_scale=v_scales[t][:],
                rhs=w_codes[h].bitcast(FP8X4),
                rhs_scale=w_scales[h][:],
                start=True,
                stop=True,
            )

        out_rows = out_0.rearrange("(p t) q -> p t q", t=PACK)
        halves = [slice(0, P), slice(P, Q)]
        copy_on = [nc.vector.tensor_copy, nc.scalar.copy]
        early = [bank([P, 3, P], "AB"[h], "early%d" % h) for h in range(2)]
        late = [bank([P, P], ("E", "S0")[h], "late%d" % h) for h in range(2)]
        for h in range(2):
            for t in range(3):
                product(early[h][:, t, :], t, h)
        for h in range(2):
            product(late[h][:], 3, h)
        for h in range(2):
            nc.scalar.copy(o_sb[:, 0:3, halves[h]], early[h][:])
        nc.sync.dma_start(out_rows[:, 0:3, :], o_sb[:, 0:3, :])
        nc.vector.tensor_copy(o_bf[:, halves[0], 0:3], o_sb[:, 0:3, halves[0]].rearrange("p t q -> p q t"))
        nc.scalar.copy(o_bf[:, halves[1], 0:3], early[1][:].rearrange("p t q -> p q t"))
        for h in range(2):
            copy_on[h](o_bf[:, halves[h], 3], late[h][:])
        quantize(o_bf[:].rearrange("p q t -> p (q t)"), o_codes[:], o_scales[:])
        for h in (1, 0):
            nc.scalar.copy(o_sb[:, 3, halves[h]], late[h][:])
        nc.scalar.dma_start(out_rows[:, 3, :], o_sb[:, 3, :])
        nc.sync.dma_start(out_1[0].rearrange("p q r -> p (q r)").bitcast(I32), o_codes[:].bitcast(I32))
        for quad in range(4):
            queue = nc.sync if quad < 2 else nc.scalar
            queue.dma_start(
                out_2[0, 4 * quad : 4 * quad + 4, :].bitcast(I32),
                o_scales[32 * quad : 32 * quad + 4, :].bitcast(I32),
            )
